import numpy as np
import ml_dtypes


def mxq(x, axis, fmt="e4m3"):
    dtype, down = {"e4m3": (ml_dtypes.float8_e4m3fn, 7), "e5m2": (ml_dtypes.float8_e5m2, 14)}[fmt]
    v = np.moveaxis(np.asarray(x, np.float32).astype(ml_dtypes.bfloat16).astype(np.float64), axis, -1)
    blocks = v.reshape(v.shape[:-1] + (-1, 32))
    amax = np.abs(blocks).max(-1, keepdims=True)
    byte = np.maximum(np.where(amax > 0, np.frexp(amax)[1] - 1 + 127, 0) - down, 1)
    scale = np.exp2(byte - 127.0)
    codes = (blocks / scale).astype(np.float32).astype(dtype).astype(np.float64)
    return np.moveaxis((codes * scale).reshape(v.shape), -1, axis)


WIDE = False


def mx_kscale(k):
    if not WIDE:
        return np.ones(k)
    levels = np.array([10, -10, 5, -5, 0])
    if k % 512:
        return np.exp2(np.random.permutation(np.resize(levels, k // 32))).repeat(32)
    a = np.empty((k // 512, 16))
    for p in range(k // 512):
        a[p, :8] = np.random.permutation(np.resize(levels, 8))
        for g in range(8):
            far = levels[np.abs(levels - a[p, g]) >= 10]
            a[p, g + 8] = far[np.random.randint(len(far))]
    return np.exp2(a.ravel()).repeat(32)


def f64(x):
    return np.asarray(x).astype(np.float64)


def striped(idx):
    return np.tile(idx.reshape(-1, 16).T, (8, 1)).astype(np.uint16)


def unstriped(offs):
    return offs[:16].T.reshape(-1).astype(np.int64)


E2M1 = np.array([0.0, 0.5, 1.0, 1.5, 2.0, 3.0, 4.0, 6.0, -0.0, -0.5, -1.0, -1.5, -2.0, -3.0, -4.0, -6.0])


def pack_weight(w, fmt):
    k, n = w.shape
    w = f64(np.asarray(w, np.float32).astype(ml_dtypes.bfloat16)).reshape(k // 32, 32, n)
    amax = np.abs(w).max(1)
    if fmt == "e4m3":
        byte = np.frexp(amax)[1] - 1 + 127 - 7
    else:
        mant, ex = np.frexp(amax / 6.0)
        byte = np.where(mant > 0.5, ex, ex - 1) + 127
    byte = np.clip(np.where(amax > 0, byte, 1), 1, 254)
    scaled = (w * np.exp2(127.0 - byte)[:, None, :]).reshape(k, n).astype(np.float32)
    by_word = np.ascontiguousarray(scaled.reshape(k // 512, 128, 4, n).transpose(0, 1, 3, 2))
    if fmt == "e4m3":
        words = by_word.astype(ml_dtypes.float8_e4m3fn).view(np.uint8)
    else:
        c = by_word.astype(ml_dtypes.float4_e2m1fn).view(np.uint8) & 0xF
        words = (c[..., 0::2] | (c[..., 1::2] << 4)).reshape(k // 512, 128, 2 * n)
    return np.ascontiguousarray(words), np.ascontiguousarray(byte.astype(np.uint8).reshape(k // 512, 16, n))


def unpack_weight(words, scales, fmt):
    g, _, n = scales.shape
    words = np.ascontiguousarray(words).reshape(g, 128, n, -1)
    if fmt == "e4m3":
        vals = words.view(ml_dtypes.float8_e4m3fn).astype(np.float64)
    else:
        nib = np.empty((g, 128, n, 4), np.uint8)
        nib[..., 0::2] = words & 0xF
        nib[..., 1::2] = words >> 4
        vals = E2M1[nib]
    vals = vals * np.repeat(np.exp2(scales.astype(np.float64) - 127.0), 8, axis=1)[..., None]
    return vals.transpose(0, 1, 3, 2).reshape(g * 512, n)


def gelu(v):
    return 0.5 * v * (1.0 + np.tanh(np.sqrt(2.0 / np.pi) * (v + 0.044715 * v**3)))


K, KA, H, T, S, T2, P, T3, S2 = 1024, 512, 1024, 2048, 1024, 2048, 512, 2048, 1024


def setup_inputs():
    n = np.random.standard_normal
    s = mx_kscale(K)[:, None]
    u = mx_kscale(H)[:, None]
    tab_words, tab_scales = pack_weight(n((K, T)) * s, "e4m3")
    w4_words, w4_scales = pack_weight(n((KA, H)) / np.sqrt(K) / s[:KA] * u.T, "e2m1")
    w1 = n((K - KA, H)) / np.sqrt(K) / s[KA:] * u.T
    tab2_words, tab2_scales = pack_weight(n((H, T3)) / np.sqrt(H) / u, "e4m3")
    return {
        "tab_words": tab_words, "tab_scales": tab_scales,
        "offs": striped(np.random.permutation(T)[:S]),
        "w4_words": w4_words, "w4_scales": w4_scales,
        "w1": w1.astype(np.float32),
        "tab2_words": tab2_words, "tab2_scales": tab2_scales,
        "offs2": striped(np.random.permutation(T3)[:S2]),
        "page0": (n((H, T2)) * u).astype(np.float32),
        "wgs": np.exp(0.3 * n((128, S))).astype(np.float32),
        "offs3": striped(np.random.permutation(T2)[:S]),
        "offs4": striped(np.random.permutation(T2)[:P]),
        "keen": np.exp(0.4 * n(P)).astype(np.float32),
        "avail": np.exp(0.4 * n((S2, P))).astype(np.float32),
    }


def reference(tab_words, tab_scales, offs, w4_words, w4_scales, w1, tab2_words, tab2_scales, offs2,
              page0, wgs, offs3, offs4, keen, avail):
    v = unpack_weight(tab_words, tab_scales, "e4m3")[:, unstriped(offs)]
    w4 = unpack_weight(w4_words, w4_scales, "e2m1")
    w1q = mxq(f64(w1), 0, "e4m3")
    h = w4.T @ v[:KA] + w1q.T @ v[KA:]
    page = f64(page0).copy()
    page[:, unstriped(offs3)] = np.tile(f64(wgs), (H // 128, 1)) * h
    x = page[:, unstriped(offs4)] * f64(keen)[None, :]
    v2 = unpack_weight(tab2_words, tab2_scales, "e4m3")[:, unstriped(offs2)]
    e = v2.T @ mxq(x, 0, "e4m3")
    return np.tanh(e * f64(avail))

@@ -1,0 +1,237 @@
+from contextlib import ExitStack
+
+import concourse.mybir as mybir
+from concourse.masks import make_identity
+
+F32 = mybir.dt.float32
+BF16 = mybir.dt.bfloat16
+I32 = mybir.dt.int32
+U32 = mybir.dt.uint32
+U16 = mybir.dt.uint16
+U8 = mybir.dt.uint8
+FP8X4 = mybir.dt.float8_e4m3fn_x4
+FP4X4 = mybir.dt.float4_e2m1fn_x4
+MULT = mybir.AluOpType.mult
+COPY = mybir.ActivationFunctionType.Copy
+TANH = mybir.ActivationFunctionType.Tanh
+
+P = 128
+H, T, S, J, S2 = 1024, 2048, 1024, 512, 1024
+BANK = 512
+FLOPS = 2 * 1024 * H * S + 2 * H * S2 * J
+W1_PIECES = ((0, 256), (256, 512), (512, 1024))
+
+
+def tile_list_wantlist_slot_matching_kernel(
+    tc, tab_words, tab_scales, offs, w4_words, w4_scales, w1, tab2_words, tab2_scales, offs2,
+    page0, wgs, offs3, offs4, keen, avail, out,
+):
+    nc = tc.nc
+    with ExitStack() as ctx:
+        lists = ctx.enter_context(tc.tile_pool(name="lists", bufs=1))
+        sb = ctx.enter_context(tc.tile_pool(name="sb", bufs=1))
+        ps = ctx.enter_context(tc.psum_pool(name="ps", bufs=1))
+
+        def held(shape, dtype, name, tag=None):
+            return sb.tile(shape, dtype, name=name, tag=tag or name, align_bytes=64)
+
+        def bank(shape, n, name):
+            return ps.tile(shape, F32, name=name, tag="bank%d" % n)
+
+        def load_list(src, name):
+            tile = lists.tile(list(src.shape), U16, name=name)
+            nc.sync.dma_start(tile[:], src)
+            return tile
+
+        def load_words(src, name, tag):
+            tile = held([P, T], U32, name, tag)
+            nc.sync.dma_start(tile[:].bitcast(I32), src.rearrange("p n t -> p (n t)").bitcast(I32))
+            return tile
+
+        def zeroed_planes(width, name):
+            tile = held([P, width], U8, name)
+            nc.vector.memset(tile[:].bitcast(I32), 0)
+            return tile
+
+        def load_planes(tile, src):
+            rows = 4 * src.shape[0]
+            for quad in range(4):
+                nc.scalar.dma_start(
+                    tile[32 * quad : 32 * quad + rows, :].bitcast(I32),
+                    src[:, 4 * quad : 4 * quad + 4, :].bitcast(I32),
+                )
+
+        def load_w1(piece):
+            c0, c1 = W1_PIECES[piece]
+            tile = held([P, 4, c1 - c0], F32, "w1_raw%d" % piece)
+            nc.sync.dma_start(tile[:], w1[:, c0:c1].rearrange("(p i) c -> p i c", i=4))
+            return tile
+
+        def quantize_w1(raw, piece):
+            c0, c1 = W1_PIECES[piece]
+            grouped = held([P, c1 - c0, 4], BF16, "w1_grouped%d" % piece)
+            nc.scalar.copy(grouped[:], raw[:].rearrange("p i c -> p c i"))
+            codes = held([P, c1 - c0], U32, "w1_codes%d" % piece)
+            scales = held([P, c1 - c0], U8, "w1_scales%d" % piece)
+            nc.vector.quantize_mx(codes[:].bitcast(FP8X4), scales[:], grouped[:].rearrange("p c i -> p (c i)"))
+            return codes, scales
+
+        def load_page(s):
+            tile = held([P, T], F32, "page%d" % s)
+            nc.sync.dma_start(tile[:], page0[P * s : P * (s + 1), :])
+            return tile
+
+        def gather(window, offsets, count, dtype, name, tag=None):
+            tile = held([P, count], dtype, name, tag)
+            nc.vector.tensor_copy(tile[:], window[:].indirect(offsets))
+            return tile
+
+        tab_planes = zeroed_planes(T, "tab_planes")
+        w4_planes = zeroed_planes(H, "w4_planes")
+        tab2_planes = zeroed_planes(T, "tab2_planes")
+        idx = load_list(offs, "idx")
+        load_planes(tab_planes, tab_scales)
+        tab_w0 = load_words(tab_words[0], "tab_w0", "words0")
+        w1_raw = [load_w1(0)]
+        tab_w1 = load_words(tab_words[1], "tab_w1", "words1")
+        load_planes(w4_planes, w4_scales)
+        w4_codes = held([P, 2 * H], U8, "w4_codes")
+        nc.sync.dma_start(w4_codes[:].bitcast(I32), w4_words[0].bitcast(I32))
+        idx3 = load_list(offs3, "idx3")
+        wgs_sb = held([P, S], F32, "wgs_sb")
+        nc.sync.dma_start(wgs_sb[:], wgs)
+        pages = [load_page(0)]
+        idx2 = load_list(offs2, "idx2")
+        load_planes(tab2_planes, tab2_scales)
+        idx4 = load_list(offs4, "idx4")
+        w1_raw.append(load_w1(1))
+        pages.append(load_page(1))
+        w1_raw.append(load_w1(2))
+        keen_sb = held([P, J // P], F32, "keen_sb")
+        with nc.allow_non_contiguous_dma(reason="one factor a partition for each chunk of 128 slots"):
+            nc.sync.dma_start(keen_sb[:], keen.rearrange("(c p) -> p c", p=P))
+        identity = held([P, P], F32, "identity")
+        make_identity(nc, identity[:])
+
+        half = S // 2
+        v_scales = gather(tab_planes, idx[:], S, U8, "v_scales")
+        v0 = [gather(tab_w0, idx[:, 32 * c : 32 * (c + 1)], half, U32, "v0_%d" % c) for c in range(2)]
+        w1_q = [quantize_w1(w1_raw[0], 0)]
+        v1 = [gather(tab_w1, idx[:, 32 * c : 32 * (c + 1)], half, U32, "v1_%d" % c) for c in range(2)]
+        v2_scales = gather(tab2_planes, idx2[:], S2, U8, "v2_scales")
+
+        tab2_w0 = load_words(tab2_words[0], "tab2_w0", "words0")
+        for s in range(2, 8):
+            pages.append(load_page(s))
+        tab2_w1 = load_words(tab2_words[1], "tab2_w1", "words1")
+        avail_sb = held([P, S2 // P, J], F32, "avail_sb")
+        nc.sync.dma_start(avail_sb[:], avail.rearrange("(m p) j -> p m j", p=P))
+
+        def make_h(s):
+            piece = [i for i, (c0, c1) in enumerate(W1_PIECES) if c0 <= P * s < c1][0]
+            codes, scales = w1_q[piece]
+            lo = P * s - W1_PIECES[piece][0]
+            h = held([P, S], F32, "h%d" % s)
+            for c in range(2):
+                cols = slice(half * c, half * (c + 1))
+                acc = bank([P, BANK], 3 + c, "h_acc")
+                nc.tensor.matmul_mx(
+                    acc[:],
+                    lhsT=w4_codes[:, 2 * P * s : 2 * P * (s + 1)].bitcast(FP4X4),
+                    lhsT_scale=w4_planes[:, P * s : P * (s + 1)],
+                    rhs=v0[c][:].bitcast(FP8X4),
+                    rhs_scale=v_scales[:, cols],
+                    start=True, stop=False,
+                )
+                nc.tensor.matmul_mx(
+                    acc[:],
+                    lhsT=codes[:, lo : lo + P].bitcast(FP8X4),
+                    lhsT_scale=scales[:, lo : lo + P],
+                    rhs=v1[c][:].bitcast(FP8X4),
+                    rhs_scale=v_scales[4:P, cols],
+                    start=False, stop=True,
+                )
+                nc.scalar.copy(h[:, cols], acc[:])
+            return h
+
+        def scatter(s, h, parts):
+            n = S // parts
+            for c in range(parts):
+                offsets = idx3[:, n // 16 * c : n // 16 * (c + 1)]
+                cols = slice(n * c, n * (c + 1))
+                nc.vector.tensor_tensor(pages[s][:].indirect(offsets), h[:, cols], wgs_sb[:, cols], MULT)
+
+        def turn_and_scale(s, picked, x_turned):
+            q = s % 4
+            turned = bank([P, 4, P], 5, "turned")
+            for c in range(4):
+                nc.tensor.transpose(turned[:, c, :], picked[:, P * c : P * (c + 1)], identity[:])
+            for c in range(4):
+                dst = x_turned[c][:].rearrange("p (u m e) -> p u m e", u=2, e=2)[:, :, 32 * q : 32 * (q + 1), :]
+                src = turned[:, c, :].rearrange("p (m u e) -> p u m e", u=2, e=2)
+                nc.scalar.activation(dst, src, COPY, scale=keen_sb[:, c : c + 1])
+
+        def turn_back(b, x_turned):
+            grouped = held([P, 4 * J], BF16, "x_grouped%d" % b)
+            pairs = grouped[:].bitcast(F32)
+            for k in range(2):
+                back = bank([P, 2, 2, P], 6 + k, "back")
+                for c in range(2):
+                    words = x_turned[2 * k + c][:].bitcast(F32)
+                    for u in range(2):
+                        nc.tensor.transpose(back[:, c, u, :], words[:, P * u : P * (u + 1)], identity[:])
+                dst = pairs[:, BANK * k : BANK * (k + 1)].rearrange("p (c j u) -> p c j u", c=2, u=2)
+                nc.scalar.copy(dst, back[:].rearrange("p c u j -> p c j u"))
+            return grouped
+
+        def quantize_x(b, grouped, tag):
+            codes = held([P, J], U32, "x_codes%d" % b, tag)
+            scales = held([P, J], U8, "x_scales%d" % b)
+            nc.vector.quantize_mx(codes[:].bitcast(FP8X4), scales[:], grouped[:])
+            return codes, scales
+
+        def score_pass(acc, m, b, v2_words, x_q):
+            cols = slice(P * m, P * (m + 1))
+            nc.tensor.matmul_mx(
+                acc[:],
+                lhsT=v2_words[:, cols].bitcast(FP8X4),
+                lhsT_scale=v2_scales[4 * b : P, cols],
+                rhs=x_q[0][:].bitcast(FP8X4),
+                rhs_scale=x_q[1][:],
+                start=(b == 0), stop=(b == 1),
+            )
+
+        hs = [make_h(0), make_h(1)]
+        x_turned = [[held([P, 4 * P], BF16, "x_turned%d_%d" % (b, c)) for c in range(4)] for b in range(2)]
+        accs = []
+        for s in range(8):
+            scatter(s, hs[s], 2 if s == 0 else 1)
+            if s == 4:
+                x0 = quantize_x(0, grouped0, "h4")
+                for m in range(5):
+                    accs.append(bank([P, BANK], m, "e_acc"))
+                    score_pass(accs[m], m, 0, v2_0, x0)
+            picked = gather(pages[s], idx4[:], J, F32, "picked%d" % s, "picked%d" % (s % 2))
+            turn_and_scale(s, picked, x_turned[s // 4])
+            if s == 0:
+                w1_q.append(quantize_w1(w1_raw[1], 1))
+                hs.extend([make_h(2), make_h(3)])
+            if s == 1:
+                w1_q.append(quantize_w1(w1_raw[2], 2))
+                hs.extend([make_h(k) for k in range(4, 8)])
+                v2_0 = gather(tab2_w0, idx2[:], S2, U32, "v2_0")
+            if s == 3:
+                grouped0 = turn_back(0, x_turned[0])
+        v2_1 = gather(tab2_w1, idx2[:], S2, U32, "v2_1", "h7")
+        grouped1 = turn_back(1, x_turned[1])
+        x1 = quantize_x(1, grouped1, None)
+        for m in range(5, 8):
+            accs.append(bank([P, BANK], m, "e_acc"))
+            score_pass(accs[m], m, 0, v2_0, x0)
+        for m in range(8):
+            score_pass(accs[m], m, 1, v2_1, x1)
+            scaled = held([P, J], F32, "scaled%d" % m, "scaled%d" % (m % 3))
+            nc.vector.tensor_tensor(scaled[:], accs[m][:], avail_sb[:, m, :], MULT)
+            result = held([P, J], F32, "result%d" % m)
+            nc.scalar.activation(result[:], scaled[:], TANH)
+            nc.sync.dma_start(out[P * m : P * (m + 1), :], result[:])

@@ -19,7 +19,7 @@ P = 128
 H, T, S, J, S2 = 1024, 2048, 1024, 512, 1024
 BANK = 512
 FLOPS = 2 * 1024 * H * S + 2 * H * S2 * J
-W1_PIECES = ((0, 256), (256, 512), (512, 1024))
+W1_PIECES = ((0, 128), (128, 512), (512, 1024))
 
 
 def tile_list_wantlist_slot_matching_kernel(
@@ -56,7 +56,7 @@ def tile_list_wantlist_slot_matching_kernel(
         def load_planes(tile, src):
             rows = 4 * src.shape[0]
             for quad in range(4):
-                nc.scalar.dma_start(
+                nc.sync.dma_start(
                     tile[32 * quad : 32 * quad + rows, :].bitcast(I32),
                     src[:, 4 * quad : 4 * quad + 4, :].bitcast(I32),
                 )
@@ -89,39 +89,46 @@ def tile_list_wantlist_slot_matching_kernel(
         tab_planes = zeroed_planes(T, "tab_planes")
         w4_planes = zeroed_planes(H, "w4_planes")
         tab2_planes = zeroed_planes(T, "tab2_planes")
+        half = S // 2
         idx = load_list(offs, "idx")
-        load_planes(tab_planes, tab_scales)
         tab_w0 = load_words(tab_words[0], "tab_w0", "words0")
-        w1_raw = [load_w1(0)]
+        load_planes(tab_planes, tab_scales)
         tab_w1 = load_words(tab_words[1], "tab_w1", "words1")
-        load_planes(w4_planes, w4_scales)
+        w1_raw = [load_w1(0)]
         w4_codes = held([P, 2 * H], U8, "w4_codes")
-        nc.sync.dma_start(w4_codes[:].bitcast(I32), w4_words[0].bitcast(I32))
-        idx3 = load_list(offs3, "idx3")
+        nc.sync.dma_start(w4_codes[:, : 2 * P].bitcast(I32), w4_words[0][:, : 2 * P].bitcast(I32))
         wgs_sb = held([P, S], F32, "wgs_sb")
-        nc.sync.dma_start(wgs_sb[:], wgs)
+        nc.sync.dma_start(wgs_sb[:, :half], wgs[:, :half])
+        load_planes(w4_planes, w4_scales)
         pages = [load_page(0)]
+        idx3 = load_list(offs3, "idx3")
+        nc.sync.dma_start(wgs_sb[:, half:], wgs[:, half:])
+        nc.sync.dma_start(w4_codes[:, 2 * P :].bitcast(I32), w4_words[0][:, 2 * P :].bitcast(I32))
+        w1_raw.append(load_w1(1))
         idx2 = load_list(offs2, "idx2")
         load_planes(tab2_planes, tab2_scales)
         idx4 = load_list(offs4, "idx4")
-        w1_raw.append(load_w1(1))
         pages.append(load_page(1))
-        w1_raw.append(load_w1(2))
         keen_sb = held([P, J // P], F32, "keen_sb")
         with nc.allow_non_contiguous_dma(reason="one factor a partition for each chunk of 128 slots"):
             nc.sync.dma_start(keen_sb[:], keen.rearrange("(c p) -> p c", p=P))
+        pages.append(load_page(2))
+        w1_raw.append(load_w1(2))
+        for s in range(3, 6):
+            pages.append(load_page(s))
         identity = held([P, P], F32, "identity")
         make_identity(nc, identity[:])
 
-        half = S // 2
+        halves = [slice(32 * c, 32 * (c + 1)) for c in range(2)]
+        v0 = [gather(tab_w0, idx[:, halves[0]], half, U32, "v0_0")]
         v_scales = gather(tab_planes, idx[:], S, U8, "v_scales")
-        v0 = [gather(tab_w0, idx[:, 32 * c : 32 * (c + 1)], half, U32, "v0_%d" % c) for c in range(2)]
+        v1 = [gather(tab_w1, idx[:, halves[0]], half, U32, "v1_0")]
         w1_q = [quantize_w1(w1_raw[0], 0)]
-        v1 = [gather(tab_w1, idx[:, 32 * c : 32 * (c + 1)], half, U32, "v1_%d" % c) for c in range(2)]
-        v2_scales = gather(tab2_planes, idx2[:], S2, U8, "v2_scales")
+        v1.append(gather(tab_w1, idx[:, halves[1]], half, U32, "v1_1", "w1_raw0"))
+        v0.append(gather(tab_w0, idx[:, halves[1]], half, U32, "v0_1", "w1_grouped0"))
 
         tab2_w0 = load_words(tab2_words[0], "tab2_w0", "words0")
-        for s in range(2, 8):
+        for s in range(6, 8):
             pages.append(load_page(s))
         tab2_w1 = load_words(tab2_words[1], "tab2_w1", "words1")
         avail_sb = held([P, S2 // P, J], F32, "avail_sb")
@@ -134,7 +141,7 @@ def tile_list_wantlist_slot_matching_kernel(
             h = held([P, S], F32, "h%d" % s)
             for c in range(2):
                 cols = slice(half * c, half * (c + 1))
-                acc = bank([P, BANK], 3 + c, "h_acc")
+                acc = bank([P, BANK], 4 + c, "h_acc")
                 nc.tensor.matmul_mx(
                     acc[:],
                     lhsT=w4_codes[:, 2 * P * s : 2 * P * (s + 1)].bitcast(FP4X4),
@@ -161,15 +168,19 @@ def tile_list_wantlist_slot_matching_kernel(
                 cols = slice(n * c, n * (c + 1))
                 nc.vector.tensor_tensor(pages[s][:].indirect(offsets), h[:, cols], wgs_sb[:, cols], MULT)
 
-        def turn_and_scale(s, picked, x_turned):
+        def pick(s, chunks, tag):
+            offsets = idx4[:, 8 * chunks.start : 8 * chunks.stop]
+            return gather(pages[s], offsets, P * len(chunks), F32, "picked", tag)
+
+        def turn_and_scale(s, chunks, picked, bank_no):
             q = s % 4
-            turned = bank([P, 4, P], 5, "turned")
-            for c in range(4):
-                nc.tensor.transpose(turned[:, c, :], picked[:, P * c : P * (c + 1)], identity[:])
-            for c in range(4):
-                dst = x_turned[c][:].rearrange("p (u m e) -> p u m e", u=2, e=2)[:, :, 32 * q : 32 * (q + 1), :]
-                src = turned[:, c, :].rearrange("p (m u e) -> p u m e", u=2, e=2)
-                nc.scalar.activation(dst, src, COPY, scale=keen_sb[:, c : c + 1])
+            turned = bank([P, len(chunks), P], bank_no, "turned")
+            for i in range(len(chunks)):
+                nc.tensor.transpose(turned[:, i, :], picked[:, P * i : P * (i + 1)], identity[:])
+            for i, c in enumerate(chunks):
+                dst = x_turned[s // 4][c][:].rearrange("p (u m e) -> p u m e", u=2, e=2)
+                src = turned[:, i, :].rearrange("p (m u e) -> p u m e", u=2, e=2)
+                nc.scalar.activation(dst[:, :, 32 * q : 32 * (q + 1), :], src, COPY, scale=keen_sb[:, c : c + 1])
 
         def turn_back(b, x_turned):
             grouped = held([P, 4 * J], BF16, "x_grouped%d" % b)
@@ -190,46 +201,61 @@ def tile_list_wantlist_slot_matching_kernel(
             nc.vector.quantize_mx(codes[:].bitcast(FP8X4), scales[:], grouped[:])
             return codes, scales
 
-        def score_pass(acc, m, b, v2_words, x_q):
+        def score_pass(acc, m, b, v2_words, x_q, first):
             cols = slice(P * m, P * (m + 1))
             nc.tensor.matmul_mx(
                 acc[:],
-                lhsT=v2_words[:, cols].bitcast(FP8X4),
+                lhsT=v2_words[m // 4][:, P * (m % 4) : P * (m % 4 + 1)].bitcast(FP8X4),
                 lhsT_scale=v2_scales[4 * b : P, cols],
                 rhs=x_q[0][:].bitcast(FP8X4),
                 rhs_scale=x_q[1][:],
-                start=(b == 0), stop=(b == 1),
+                start=first, stop=not first,
             )
 
-        hs = [make_h(0), make_h(1)]
         x_turned = [[held([P, 4 * P], BF16, "x_turned%d_%d" % (b, c)) for c in range(4)] for b in range(2)]
-        accs = []
-        for s in range(8):
-            scatter(s, hs[s], 2 if s == 0 else 1)
-            if s == 4:
-                x0 = quantize_x(0, grouped0, "h4")
-                for m in range(5):
-                    accs.append(bank([P, BANK], m, "e_acc"))
-                    score_pass(accs[m], m, 0, v2_0, x0)
-            picked = gather(pages[s], idx4[:], J, F32, "picked%d" % s, "picked%d" % (s % 2))
-            turn_and_scale(s, picked, x_turned[s // 4])
-            if s == 0:
-                w1_q.append(quantize_w1(w1_raw[1], 1))
-                hs.extend([make_h(2), make_h(3)])
+        every = range(4)
+        ring = "w1_grouped1"
+        scatter(0, make_h(0), 2)
+        w1_q.append(quantize_w1(w1_raw[1], 1))
+        v2_scales = gather(tab2_planes, idx2[:], S2, U8, "v2_scales", "w1_raw1")
+        h = make_h(1)
+        picked = pick(0, every, ring)
+        scatter(1, h, 1)
+        for s in range(1, 6):
+            h = make_h(s + 1)
+            turn_and_scale(s - 1, every, picked, 5)
+            scatter(s + 1, h, 1)
+            picked = pick(s, every, ring)
             if s == 1:
                 w1_q.append(quantize_w1(w1_raw[2], 2))
-                hs.extend([make_h(k) for k in range(4, 8)])
-                v2_0 = gather(tab2_w0, idx2[:], S2, U32, "v2_0")
-            if s == 3:
+            if s == 4:
                 grouped0 = turn_back(0, x_turned[0])
-        v2_1 = gather(tab2_w1, idx2[:], S2, U32, "v2_1", "h7")
+        picked6 = pick(6, every, "picked6")
+        h = make_h(7)
+        turn_and_scale(5, every, picked, 5)
+        turn_and_scale(6, every, picked6, 4)
+        scatter(7, h, 1)
+        x0 = quantize_x(0, grouped0, ring)
+        for k in range(2):
+            chunks = range(2 * k, 2 * k + 2)
+            turn_and_scale(7, chunks, pick(7, chunks, "picked7_%d" % k), 4 + k)
+        v2_early = held([P, S2 + half], U32, "v2_early", "page7")
+        nc.vector.tensor_copy(v2_early[:, :S2], tab2_w1[:].indirect(idx2[:]))
+        nc.vector.tensor_copy(v2_early[:, S2:], tab2_w0[:].indirect(idx2[:, halves[0]]))
+        v2_1 = [v2_early[:, :half], v2_early[:, half:S2]]
+        v2_0 = [v2_early[:, S2:]]
         grouped1 = turn_back(1, x_turned[1])
         x1 = quantize_x(1, grouped1, None)
-        for m in range(5, 8):
-            accs.append(bank([P, BANK], m, "e_acc"))
-            score_pass(accs[m], m, 0, v2_0, x0)
+        v2_0.append(gather(tab2_w0, idx2[:, halves[1]], half, U32, "v2_0b", "x_grouped1")[:])
+        accs = [bank([P, BANK], (6 + m) % 8, "e_acc") for m in range(8)]
+        for m in range(2):
+            score_pass(accs[m], m, 0, v2_0, x0, True)
         for m in range(8):
-            score_pass(accs[m], m, 1, v2_1, x1)
+            if m < 2:
+                score_pass(accs[m], m, 1, v2_1, x1, False)
+            else:
+                score_pass(accs[m], m, 1, v2_1, x1, True)
+                score_pass(accs[m], m, 0, v2_0, x0, False)
             scaled = held([P, J], F32, "scaled%d" % m, "scaled%d" % (m % 3))
             nc.vector.tensor_tensor(scaled[:], accs[m][:], avail_sb[:, m, :], MULT)
             result = held([P, J], F32, "result%d" % m)

@@ -19,7 +19,7 @@ P = 128
 H, T, S, J, S2 = 1024, 2048, 1024, 512, 1024
 BANK = 512
 FLOPS = 2 * 1024 * H * S + 2 * H * S2 * J
-W1_PIECES = ((0, 128), (128, 512), (512, 1024))
+W1_PIECES = ((0, 128), (128, 256), (256, 512), (512, 1024))
 
 
 def tile_list_wantlist_slot_matching_kernel(
@@ -48,9 +48,9 @@ def tile_list_wantlist_slot_matching_kernel(
             nc.sync.dma_start(tile[:].bitcast(I32), src.rearrange("p n t -> p (n t)").bitcast(I32))
             return tile
 
-        def zeroed_planes(width, name):
+        def zeroed_planes(width, name, engine):
             tile = held([P, width], U8, name)
-            nc.vector.memset(tile[:].bitcast(I32), 0)
+            engine.memset(tile[:].bitcast(I32), 0)
             return tile
 
         def load_planes(tile, src):
@@ -76,9 +76,17 @@ def tile_list_wantlist_slot_matching_kernel(
             nc.vector.quantize_mx(codes[:].bitcast(FP8X4), scales[:], grouped[:].rearrange("p c i -> p (c i)"))
             return codes, scales
 
+        w4_codes = held([P, 2 * H], U8, "w4_codes")
+
+        def load_w4(s):
+            cols = slice(2 * P * s, 2 * P * (s + 1))
+            nc.sync.dma_start(w4_codes[:, cols].bitcast(I32), w4_words[0][:, cols].bitcast(I32))
+
         def load_page(s):
             tile = held([P, T], F32, "page%d" % s)
             nc.sync.dma_start(tile[:], page0[P * s : P * (s + 1), :])
+            if s > 0:
+                load_w4(s)
             return tile
 
         def gather(window, offsets, count, dtype, name, tag=None):
@@ -86,46 +94,44 @@ def tile_list_wantlist_slot_matching_kernel(
             nc.vector.tensor_copy(tile[:], window[:].indirect(offsets))
             return tile
 
-        tab_planes = zeroed_planes(T, "tab_planes")
-        w4_planes = zeroed_planes(H, "w4_planes")
-        tab2_planes = zeroed_planes(T, "tab2_planes")
+        tab_planes = zeroed_planes(T, "tab_planes", nc.gpsimd)
+        w4_planes = zeroed_planes(H, "w4_planes", nc.vector)
+        tab2_planes = zeroed_planes(T, "tab2_planes", nc.vector)
         half = S // 2
         idx = load_list(offs, "idx")
-        tab_w0 = load_words(tab_words[0], "tab_w0", "words0")
-        load_planes(tab_planes, tab_scales)
-        tab_w1 = load_words(tab_words[1], "tab_w1", "words1")
         w1_raw = [load_w1(0)]
-        w4_codes = held([P, 2 * H], U8, "w4_codes")
-        nc.sync.dma_start(w4_codes[:, : 2 * P].bitcast(I32), w4_words[0][:, : 2 * P].bitcast(I32))
+        load_planes(tab_planes, tab_scales)
+        tab_w0 = load_words(tab_words[0], "tab_w0", "words0")
+        tab_w1 = load_words(tab_words[1], "tab_w1", "words1")
+        load_w4(0)
         wgs_sb = held([P, S], F32, "wgs_sb")
         nc.sync.dma_start(wgs_sb[:, :half], wgs[:, :half])
         load_planes(w4_planes, w4_scales)
-        pages = [load_page(0)]
-        idx3 = load_list(offs3, "idx3")
-        nc.sync.dma_start(wgs_sb[:, half:], wgs[:, half:])
-        nc.sync.dma_start(w4_codes[:, 2 * P :].bitcast(I32), w4_words[0][:, 2 * P :].bitcast(I32))
         w1_raw.append(load_w1(1))
         idx2 = load_list(offs2, "idx2")
         load_planes(tab2_planes, tab2_scales)
+        pages = [load_page(0)]
+        idx3 = load_list(offs3, "idx3")
+        nc.sync.dma_start(wgs_sb[:, half:], wgs[:, half:])
+        w1_raw.append(load_w1(2))
+        pages.extend([load_page(1), load_page(2)])
         idx4 = load_list(offs4, "idx4")
-        pages.append(load_page(1))
         keen_sb = held([P, J // P], F32, "keen_sb")
         with nc.allow_non_contiguous_dma(reason="one factor a partition for each chunk of 128 slots"):
             nc.sync.dma_start(keen_sb[:], keen.rearrange("(c p) -> p c", p=P))
-        pages.append(load_page(2))
-        w1_raw.append(load_w1(2))
+        w1_raw.append(load_w1(3))
         for s in range(3, 6):
             pages.append(load_page(s))
         identity = held([P, P], F32, "identity")
         make_identity(nc, identity[:])
 
         halves = [slice(32 * c, 32 * (c + 1)) for c in range(2)]
-        v0 = [gather(tab_w0, idx[:, halves[0]], half, U32, "v0_0")]
         v_scales = gather(tab_planes, idx[:], S, U8, "v_scales")
-        v1 = [gather(tab_w1, idx[:, halves[0]], half, U32, "v1_0")]
         w1_q = [quantize_w1(w1_raw[0], 0)]
-        v1.append(gather(tab_w1, idx[:, halves[1]], half, U32, "v1_1", "w1_raw0"))
-        v0.append(gather(tab_w0, idx[:, halves[1]], half, U32, "v0_1", "w1_grouped0"))
+        v0 = gather(tab_w0, idx[:], S, U32, "v0")
+        v1 = gather(tab_w1, idx[:], S, U32, "v1")
+        w1_q.append(quantize_w1(w1_raw[1], 1))
+        v2_scales = gather(tab2_planes, idx2[:], S2, U8, "v2_scales")
 
         tab2_w0 = load_words(tab2_words[0], "tab2_w0", "words0")
         for s in range(6, 8):
@@ -146,7 +152,7 @@ def tile_list_wantlist_slot_matching_kernel(
                     acc[:],
                     lhsT=w4_codes[:, 2 * P * s : 2 * P * (s + 1)].bitcast(FP4X4),
                     lhsT_scale=w4_planes[:, P * s : P * (s + 1)],
-                    rhs=v0[c][:].bitcast(FP8X4),
+                    rhs=v0[:, cols].bitcast(FP8X4),
                     rhs_scale=v_scales[:, cols],
                     start=True, stop=False,
                 )
@@ -154,7 +160,7 @@ def tile_list_wantlist_slot_matching_kernel(
                     acc[:],
                     lhsT=codes[:, lo : lo + P].bitcast(FP8X4),
                     lhsT_scale=scales[:, lo : lo + P],
-                    rhs=v1[c][:].bitcast(FP8X4),
+                    rhs=v1[:, cols].bitcast(FP8X4),
                     rhs_scale=v_scales[4:P, cols],
                     start=False, stop=True,
                 )
@@ -185,14 +191,13 @@ def tile_list_wantlist_slot_matching_kernel(
         def turn_back(b, x_turned):
             grouped = held([P, 4 * J], BF16, "x_grouped%d" % b)
             pairs = grouped[:].bitcast(F32)
-            for k in range(2):
-                back = bank([P, 2, 2, P], 6 + k, "back")
-                for c in range(2):
-                    words = x_turned[2 * k + c][:].bitcast(F32)
-                    for u in range(2):
-                        nc.tensor.transpose(back[:, c, u, :], words[:, P * u : P * (u + 1)], identity[:])
-                dst = pairs[:, BANK * k : BANK * (k + 1)].rearrange("p (c j u) -> p c j u", c=2, u=2)
-                nc.scalar.copy(dst, back[:].rearrange("p c u j -> p c j u"))
+            for c in range(4):
+                back = bank([P, 2, P], (6 + c) % 8, "back")
+                words = x_turned[c][:].bitcast(F32)
+                for u in range(2):
+                    nc.tensor.transpose(back[:, u, :], words[:, P * u : P * (u + 1)], identity[:])
+                dst = pairs[:, 2 * P * c : 2 * P * (c + 1)].rearrange("p (j u) -> p j u", u=2)
+                nc.scalar.copy(dst, back[:].rearrange("p u j -> p j u"))
             return grouped
 
         def quantize_x(b, grouped, tag):
@@ -214,50 +219,49 @@ def tile_list_wantlist_slot_matching_kernel(
 
         x_turned = [[held([P, 4 * P], BF16, "x_turned%d_%d" % (b, c)) for c in range(4)] for b in range(2)]
         every = range(4)
-        ring = "w1_grouped1"
+        ring = "picked"
         scatter(0, make_h(0), 2)
-        w1_q.append(quantize_w1(w1_raw[1], 1))
-        v2_scales = gather(tab2_planes, idx2[:], S2, U8, "v2_scales", "w1_raw1")
-        h = make_h(1)
+        w1_q.append(quantize_w1(w1_raw[2], 2))
+        scatter(1, make_h(1), 1)
         picked = pick(0, every, ring)
-        scatter(1, h, 1)
         for s in range(1, 6):
             h = make_h(s + 1)
             turn_and_scale(s - 1, every, picked, 5)
             scatter(s + 1, h, 1)
             picked = pick(s, every, ring)
             if s == 1:
-                w1_q.append(quantize_w1(w1_raw[2], 2))
+                w1_q.append(quantize_w1(w1_raw[3], 3))
             if s == 4:
                 grouped0 = turn_back(0, x_turned[0])
         picked6 = pick(6, every, "picked6")
         h = make_h(7)
         turn_and_scale(5, every, picked, 5)
-        turn_and_scale(6, every, picked6, 4)
+        turn_and_scale(6, every, picked6, 5)
         scatter(7, h, 1)
         x0 = quantize_x(0, grouped0, ring)
         for k in range(2):
             chunks = range(2 * k, 2 * k + 2)
             turn_and_scale(7, chunks, pick(7, chunks, "picked7_%d" % k), 4 + k)
-        v2_early = held([P, S2 + half], U32, "v2_early", "page7")
-        nc.vector.tensor_copy(v2_early[:, :S2], tab2_w1[:].indirect(idx2[:]))
-        nc.vector.tensor_copy(v2_early[:, S2:], tab2_w0[:].indirect(idx2[:, halves[0]]))
-        v2_1 = [v2_early[:, :half], v2_early[:, half:S2]]
-        v2_0 = [v2_early[:, S2:]]
+        v2_0 = [gather(tab2_w0, idx2[:, halves[0]], half, U32, "v2_0a", "x_grouped0")[:]]
+        v2_1 = gather(tab2_w1, idx2[:], S2, U32, "v2_1", "page7")
+        v2_1 = [v2_1[:, :half], v2_1[:, half:]]
         grouped1 = turn_back(1, x_turned[1])
         x1 = quantize_x(1, grouped1, None)
         v2_0.append(gather(tab2_w0, idx2[:, halves[1]], half, U32, "v2_0b", "x_grouped1")[:])
         accs = [bank([P, BANK], (6 + m) % 8, "e_acc") for m in range(8)]
-        for m in range(2):
+        for m in range(4):
             score_pass(accs[m], m, 0, v2_0, x0, True)
         for m in range(8):
-            if m < 2:
+            if m < 4:
                 score_pass(accs[m], m, 1, v2_1, x1, False)
             else:
                 score_pass(accs[m], m, 1, v2_1, x1, True)
                 score_pass(accs[m], m, 0, v2_0, x0, False)
-            scaled = held([P, J], F32, "scaled%d" % m, "scaled%d" % (m % 3))
-            nc.vector.tensor_tensor(scaled[:], accs[m][:], avail_sb[:, m, :], MULT)
-            result = held([P, J], F32, "result%d" % m)
-            nc.scalar.activation(result[:], scaled[:], TANH)
-            nc.sync.dma_start(out[P * m : P * (m + 1), :], result[:])
+            parts = 2 if m == 7 else 1
+            for k in range(parts):
+                cols = slice(J // parts * k, J // parts * (k + 1))
+                scaled = held([P, J // parts], F32, "scaled", "scaled%d" % ((m + k) % 3))
+                nc.vector.tensor_tensor(scaled[:], accs[m][:, cols], avail_sb[:, m, cols], MULT)
+                result = held([P, J // parts], F32, "result%d_%d" % (m, k))
+                nc.scalar.activation(result[:], scaled[:], TANH)
+                nc.sync.dma_start(out[P * m : P * (m + 1), cols], result[:])

from contextlib import ExitStack

import concourse.mybir as mybir
from concourse.masks import make_identity

F32 = mybir.dt.float32
BF16 = mybir.dt.bfloat16
I32 = mybir.dt.int32
U32 = mybir.dt.uint32
U16 = mybir.dt.uint16
U8 = mybir.dt.uint8
FP8X4 = mybir.dt.float8_e4m3fn_x4
FP4X4 = mybir.dt.float4_e2m1fn_x4
MULT = mybir.AluOpType.mult
COPY = mybir.ActivationFunctionType.Copy
TANH = mybir.ActivationFunctionType.Tanh

P = 128
H, T, S, J, S2 = 1024, 2048, 1024, 512, 1024
BANK = 512
FLOPS = 2 * 1024 * H * S + 2 * H * S2 * J
W1_PIECES = ((0, 128), (128, 256), (256, 512), (512, 1024))


def tile_list_wantlist_slot_matching_kernel(
    tc, tab_words, tab_scales, offs, w4_words, w4_scales, w1, tab2_words, tab2_scales, offs2,
    page0, wgs, offs3, offs4, keen, avail, out,
):
    nc = tc.nc
    with ExitStack() as ctx:
        lists = ctx.enter_context(tc.tile_pool(name="lists", bufs=1))
        sb = ctx.enter_context(tc.tile_pool(name="sb", bufs=1))
        ps = ctx.enter_context(tc.psum_pool(name="ps", bufs=1))

        def held(shape, dtype, name, tag=None):
            return sb.tile(shape, dtype, name=name, tag=tag or name, align_bytes=64)

        def bank(shape, n, name):
            return ps.tile(shape, F32, name=name, tag="bank%d" % n)

        def load_list(src, name):
            tile = lists.tile(list(src.shape), U16, name=name)
            nc.sync.dma_start(tile[:], src)
            return tile

        def load_words(src, name, tag):
            tile = held([P, T], U32, name, tag)
            nc.sync.dma_start(tile[:].bitcast(I32), src.rearrange("p n t -> p (n t)").bitcast(I32))
            return tile

        def zeroed_planes(width, name, engine):
            tile = held([P, width], U8, name)
            engine.memset(tile[:].bitcast(I32), 0)
            return tile

        def load_planes(tile, src):
            rows = 4 * src.shape[0]
            for quad in range(4):
                nc.sync.dma_start(
                    tile[32 * quad : 32 * quad + rows, :].bitcast(I32),
                    src[:, 4 * quad : 4 * quad + 4, :].bitcast(I32),
                )

        def load_w1(piece):
            c0, c1 = W1_PIECES[piece]
            tile = held([P, 4, c1 - c0], F32, "w1_raw%d" % piece)
            nc.sync.dma_start(tile[:], w1[:, c0:c1].rearrange("(p i) c -> p i c", i=4))
            return tile

        def quantize_w1(raw, piece):
            c0, c1 = W1_PIECES[piece]
            grouped = held([P, c1 - c0, 4], BF16, "w1_grouped%d" % piece)
            nc.scalar.copy(grouped[:], raw[:].rearrange("p i c -> p c i"))
            codes = held([P, c1 - c0], U32, "w1_codes%d" % piece)
            scales = held([P, c1 - c0], U8, "w1_scales%d" % piece)
            nc.vector.quantize_mx(codes[:].bitcast(FP8X4), scales[:], grouped[:].rearrange("p c i -> p (c i)"))
            return codes, scales

        w4_codes = held([P, 2 * H], U8, "w4_codes")

        def load_w4(s):
            cols = slice(2 * P * s, 2 * P * (s + 1))
            nc.sync.dma_start(w4_codes[:, cols].bitcast(I32), w4_words[0][:, cols].bitcast(I32))

        def load_page(s):
            tile = held([P, T], F32, "page%d" % s)
            nc.sync.dma_start(tile[:], page0[P * s : P * (s + 1), :])
            if s > 0:
                load_w4(s)
            return tile

        def gather(window, offsets, count, dtype, name, tag=None):
            tile = held([P, count], dtype, name, tag)
            nc.vector.tensor_copy(tile[:], window[:].indirect(offsets))
            return tile

        tab_planes = zeroed_planes(T, "tab_planes", nc.gpsimd)
        w4_planes = zeroed_planes(H, "w4_planes", nc.vector)
        tab2_planes = zeroed_planes(T, "tab2_planes", nc.vector)
        half = S // 2
        idx = load_list(offs, "idx")
        w1_raw = [load_w1(0)]
        load_planes(tab_planes, tab_scales)
        tab_w0 = load_words(tab_words[0], "tab_w0", "words0")
        tab_w1 = load_words(tab_words[1], "tab_w1", "words1")
        load_w4(0)
        wgs_sb = held([P, S], F32, "wgs_sb")
        nc.sync.dma_start(wgs_sb[:, :half], wgs[:, :half])
        load_planes(w4_planes, w4_scales)
        w1_raw.append(load_w1(1))
        idx2 = load_list(offs2, "idx2")
        load_planes(tab2_planes, tab2_scales)
        pages = [load_page(0)]
        idx3 = load_list(offs3, "idx3")
        nc.sync.dma_start(wgs_sb[:, half:], wgs[:, half:])
        w1_raw.append(load_w1(2))
        pages.extend([load_page(1), load_page(2)])
        idx4 = load_list(offs4, "idx4")
        keen_sb = held([P, J // P], F32, "keen_sb")
        with nc.allow_non_contiguous_dma(reason="one factor a partition for each chunk of 128 slots"):
            nc.sync.dma_start(keen_sb[:], keen.rearrange("(c p) -> p c", p=P))
        w1_raw.append(load_w1(3))
        for s in range(3, 6):
            pages.append(load_page(s))
        identity = held([P, P], F32, "identity")
        make_identity(nc, identity[:])

        halves = [slice(32 * c, 32 * (c + 1)) for c in range(2)]
        v_scales = gather(tab_planes, idx[:], S, U8, "v_scales")
        w1_q = [quantize_w1(w1_raw[0], 0)]
        v0 = gather(tab_w0, idx[:], S, U32, "v0")
        v1 = gather(tab_w1, idx[:], S, U32, "v1")
        w1_q.append(quantize_w1(w1_raw[1], 1))
        v2_scales = gather(tab2_planes, idx2[:], S2, U8, "v2_scales")

        tab2_w0 = load_words(tab2_words[0], "tab2_w0", "words0")
        for s in range(6, 8):
            pages.append(load_page(s))
        tab2_w1 = load_words(tab2_words[1], "tab2_w1", "words1")
        avail_sb = held([P, S2 // P, J], F32, "avail_sb")
        nc.sync.dma_start(avail_sb[:], avail.rearrange("(m p) j -> p m j", p=P))

        def make_h(s):
            piece = [i for i, (c0, c1) in enumerate(W1_PIECES) if c0 <= P * s < c1][0]
            codes, scales = w1_q[piece]
            lo = P * s - W1_PIECES[piece][0]
            h = held([P, S], F32, "h%d" % s)
            for c in range(2):
                cols = slice(half * c, half * (c + 1))
                acc = bank([P, BANK], 4 + c, "h_acc")
                nc.tensor.matmul_mx(
                    acc[:],
                    lhsT=w4_codes[:, 2 * P * s : 2 * P * (s + 1)].bitcast(FP4X4),
                    lhsT_scale=w4_planes[:, P * s : P * (s + 1)],
                    rhs=v0[:, cols].bitcast(FP8X4),
                    rhs_scale=v_scales[:, cols],
                    start=True, stop=False,
                )
                nc.tensor.matmul_mx(
                    acc[:],
                    lhsT=codes[:, lo : lo + P].bitcast(FP8X4),
                    lhsT_scale=scales[:, lo : lo + P],
                    rhs=v1[:, cols].bitcast(FP8X4),
                    rhs_scale=v_scales[4:P, cols],
                    start=False, stop=True,
                )
                nc.scalar.copy(h[:, cols], acc[:])
            return h

        def scatter(s, h, parts):
            n = S // parts
            for c in range(parts):
                offsets = idx3[:, n // 16 * c : n // 16 * (c + 1)]
                cols = slice(n * c, n * (c + 1))
                nc.vector.tensor_tensor(pages[s][:].indirect(offsets), h[:, cols], wgs_sb[:, cols], MULT)

        def pick(s, chunks, tag):
            offsets = idx4[:, 8 * chunks.start : 8 * chunks.stop]
            return gather(pages[s], offsets, P * len(chunks), F32, "picked", tag)

        def turn_and_scale(s, chunks, picked, bank_no):
            q = s % 4
            turned = bank([P, len(chunks), P], bank_no, "turned")
            for i in range(len(chunks)):
                nc.tensor.transpose(turned[:, i, :], picked[:, P * i : P * (i + 1)], identity[:])
            for i, c in enumerate(chunks):
                dst = x_turned[s // 4][c][:].rearrange("p (u m e) -> p u m e", u=2, e=2)
                src = turned[:, i, :].rearrange("p (m u e) -> p u m e", u=2, e=2)
                nc.scalar.activation(dst[:, :, 32 * q : 32 * (q + 1), :], src, COPY, scale=keen_sb[:, c : c + 1])

        def turn_back(b, x_turned):
            grouped = held([P, 4 * J], BF16, "x_grouped%d" % b)
            pairs = grouped[:].bitcast(F32)
            for c in range(4):
                back = bank([P, 2, P], (6 + c) % 8, "back")
                words = x_turned[c][:].bitcast(F32)
                for u in range(2):
                    nc.tensor.transpose(back[:, u, :], words[:, P * u : P * (u + 1)], identity[:])
                dst = pairs[:, 2 * P * c : 2 * P * (c + 1)].rearrange("p (j u) -> p j u", u=2)
                nc.scalar.copy(dst, back[:].rearrange("p u j -> p j u"))
            return grouped

        def quantize_x(b, grouped, tag):
            codes = held([P, J], U32, "x_codes%d" % b, tag)
            scales = held([P, J], U8, "x_scales%d" % b)
            nc.vector.quantize_mx(codes[:].bitcast(FP8X4), scales[:], grouped[:])
            return codes, scales

        def score_pass(acc, m, b, v2_words, x_q, first):
            cols = slice(P * m, P * (m + 1))
            nc.tensor.matmul_mx(
                acc[:],
                lhsT=v2_words[m // 4][:, P * (m % 4) : P * (m % 4 + 1)].bitcast(FP8X4),
                lhsT_scale=v2_scales[4 * b : P, cols],
                rhs=x_q[0][:].bitcast(FP8X4),
                rhs_scale=x_q[1][:],
                start=first, stop=not first,
            )

        x_turned = [[held([P, 4 * P], BF16, "x_turned%d_%d" % (b, c)) for c in range(4)] for b in range(2)]
        every = range(4)
        ring = "picked"
        scatter(0, make_h(0), 2)
        w1_q.append(quantize_w1(w1_raw[2], 2))
        scatter(1, make_h(1), 1)
        picked = pick(0, every, ring)
        for s in range(1, 6):
            h = make_h(s + 1)
            turn_and_scale(s - 1, every, picked, 5)
            scatter(s + 1, h, 1)
            picked = pick(s, every, ring)
            if s == 1:
                w1_q.append(quantize_w1(w1_raw[3], 3))
            if s == 4:
                grouped0 = turn_back(0, x_turned[0])
        picked6 = pick(6, every, "picked6")
        h = make_h(7)
        turn_and_scale(5, every, picked, 5)
        turn_and_scale(6, every, picked6, 5)
        scatter(7, h, 1)
        x0 = quantize_x(0, grouped0, ring)
        for k in range(2):
            chunks = range(2 * k, 2 * k + 2)
            turn_and_scale(7, chunks, pick(7, chunks, "picked7_%d" % k), 4 + k)
        v2_0 = [gather(tab2_w0, idx2[:, halves[0]], half, U32, "v2_0a", "x_grouped0")[:]]
        v2_1 = gather(tab2_w1, idx2[:], S2, U32, "v2_1", "page7")
        v2_1 = [v2_1[:, :half], v2_1[:, half:]]
        grouped1 = turn_back(1, x_turned[1])
        x1 = quantize_x(1, grouped1, None)
        v2_0.append(gather(tab2_w0, idx2[:, halves[1]], half, U32, "v2_0b", "x_grouped1")[:])
        accs = [bank([P, BANK], (6 + m) % 8, "e_acc") for m in range(8)]
        for m in range(4):
            score_pass(accs[m], m, 0, v2_0, x0, True)
        for m in range(8):
            if m < 4:
                score_pass(accs[m], m, 1, v2_1, x1, False)
            else:
                score_pass(accs[m], m, 1, v2_1, x1, True)
                score_pass(accs[m], m, 0, v2_0, x0, False)
            parts = 2 if m == 7 else 1
            for k in range(parts):
                cols = slice(J // parts * k, J // parts * (k + 1))
                scaled = held([P, J // parts], F32, "scaled", "scaled%d" % ((m + k) % 3))
                nc.vector.tensor_tensor(scaled[:], accs[m][:, cols], avail_sb[:, m, cols], MULT)
                result = held([P, J // parts], F32, "result%d_%d" % (m, k))
                nc.scalar.activation(result[:], scaled[:], TANH)
                nc.sync.dma_start(out[P * m : P * (m + 1), cols], result[:])
